import numpy as np
import ml_dtypes


def mxq(x, axis, fmt="e4m3"):
    dtype, down = {"e4m3": (ml_dtypes.float8_e4m3fn, 7), "e5m2": (ml_dtypes.float8_e5m2, 14)}[fmt]
    v = np.moveaxis(np.asarray(x, np.float32).astype(ml_dtypes.bfloat16).astype(np.float64), axis, -1)
    blocks = v.reshape(v.shape[:-1] + (-1, 32))
    amax = np.abs(blocks).max(-1, keepdims=True)
    byte = np.maximum(np.where(amax > 0, np.frexp(amax)[1] - 1 + 127, 0) - down, 1)
    scale = np.exp2(byte - 127.0)
    codes = (blocks / scale).astype(np.float32).astype(dtype).astype(np.float64)
    return np.moveaxis((codes * scale).reshape(v.shape), -1, axis)


WIDE = False


def mx_kscale(k):
    if not WIDE:
        return np.ones(k)
    levels = np.array([10, -10, 5, -5, 0])
    if k % 512:
        return np.exp2(np.random.permutation(np.resize(levels, k // 32))).repeat(32)
    a = np.empty((k // 512, 16))
    for p in range(k // 512):
        a[p, :8] = np.random.permutation(np.resize(levels, 8))
        for g in range(8):
            far = levels[np.abs(levels - a[p, g]) >= 10]
            a[p, g + 8] = far[np.random.randint(len(far))]
    return np.exp2(a.ravel()).repeat(32)


def f64(x):
    return np.asarray(x).astype(np.float64)


def striped(idx):
    return np.tile(idx.reshape(-1, 16).T, (8, 1)).astype(np.uint16)


def unstriped(offs):
    return offs[:16].T.reshape(-1).astype(np.int64)


def pack_weight(w):
    k, n = w.shape
    w = f64(np.asarray(w, np.float32).astype(ml_dtypes.bfloat16)).reshape(k // 32, 32, n)
    amax = np.abs(w).max(1)
    byte = np.clip(np.where(amax > 0, np.frexp(amax)[1] - 1 + 127 - 7, 1), 1, 254)
    scaled = (w * np.exp2(127.0 - byte)[:, None, :]).reshape(k, n).astype(np.float32)
    words = np.ascontiguousarray(scaled.reshape(k // 512, 128, 4, n).transpose(0, 1, 3, 2)).astype(ml_dtypes.float8_e4m3fn).view(np.uint8)
    return words, np.ascontiguousarray(byte.astype(np.uint8).reshape(k // 512, 16, n))


def unpack_weight(words, scales):
    g, p, n, _ = words.shape
    vals = np.ascontiguousarray(words).view(ml_dtypes.float8_e4m3fn).astype(np.float64) * np.repeat(np.exp2(scales.astype(np.float64) - 127.0), 8, axis=1)[..., None]
    return vals.transpose(0, 1, 3, 2).reshape(g * 512, n)


K, T, S, N, H, U = 512, 2048, 512, 128, 512, 1024


def setup_inputs():
    n = np.random.standard_normal
    s = mx_kscale(K)[:, None]
    u = mx_kscale(H)
    packed_xT = pack_weight(n((K, T)) * s)
    return {
        "x_words": packed_xT[0],
        "x_scales": packed_xT[1],
        "w1": (n((K, H)) / np.sqrt(K) / s).astype(np.float32),
        "unit": (np.random.uniform(0.6, 1.4, (H, 1)) * u[:, None]).astype(np.float32),
        "w2": (n((H, N)) / np.sqrt(H) / u[:, None]).astype(np.float32),
        "offs": striped(np.random.permutation(T)[:S]),
        "nu": striped(np.random.permutation(np.concatenate([np.arange(S), np.random.randint(0, S, U - S)]))),
        "el": striped(np.random.permutation(np.concatenate([np.arange(S), np.random.randint(0, S, U - S)]))),
        "ct": striped(np.random.permutation(np.concatenate([np.arange(S), np.random.randint(0, S, U - S)]))),
    }


def reference(x_words, x_scales, w1, unit, w2, offs, nu, el, ct):
    xq = unpack_weight(x_words, x_scales)[:, unstriped(offs)]
    y = mxq(f64(w1), 0, "e4m3").T @ xq
    yn = y[:, unstriped(nu)]
    ye1 = y[:, unstriped(el)]
    chg = yn * ye1
    yc2 = y[:, unstriped(ct)]
    hid = f64(unit) * (chg / (np.abs(yc2) + 0.6) - yn)
    return mxq(f64(w2), 0, "e4m3").T @ mxq(hid, 0, "e4m3")

@@ -1,0 +1,165 @@
+from contextlib import ExitStack
+
+import concourse.mybir as mybir
+
+K, T, S, N, H, U = 512, 2048, 512, 128, 512, 1024
+FLOPS = 2 * K * H * S + 2 * H * N * U
+
+F32 = mybir.dt.float32
+BF16 = mybir.dt.bfloat16
+I32 = mybir.dt.int32
+U32 = mybir.dt.uint32
+U16 = mybir.dt.uint16
+U8 = mybir.dt.uint8
+FP8X4 = mybir.dt.float8_e4m3fn_x4
+ALU = mybir.AluOpType
+ACT = mybir.ActivationFunctionType
+
+P = 128
+PACK = 4
+CHUNKS = (384, 384, 128, 128)
+MM_WIDTHS = {384: (256, 128), 256: (256,), 128: (128,)}
+VECTOR_GATHERS = ((0, 0),)
+
+
+def tile_picked_ypartnr_cat_p_kernel(tc, x_words, x_scales, w1, unit, w2, offs, nu, el, ct, out):
+    nc = tc.nc
+    with ExitStack() as ctx:
+        keep = ctx.enter_context(tc.tile_pool(name="keep", bufs=1))
+        work = ctx.enter_context(tc.tile_pool(name="work", bufs=2))
+        psum = ctx.enter_context(tc.psum_pool(name="psum", bufs=1))
+
+        offs_sb = keep.tile([P, S // 16], U16, name="offs_sb")
+        nu_sb = keep.tile([P, U // 16], U16, name="nu_sb")
+        el_sb = keep.tile([P, U // 16], U16, name="el_sb")
+        ct_sb = keep.tile([P, U // 16], U16, name="ct_sb")
+        x_table = keep.tile([P, T], I32, name="x_table", align_bytes=64)
+        scale_table = keep.tile([P, T], U8, name="scale_table", align_bytes=64)
+        unit_sb = keep.tile([P, PACK], F32, name="unit_sb")
+
+        nc.vector.memset(scale_table[:].bitcast(I32), 0)
+        nc.sync.dma_start(offs_sb[:], offs)
+        half = H // 2
+        w1_raw = []
+        for h in range(2):
+            raw = keep.tile([P, PACK, half], F32, name="w1_raw%d" % h)
+            nc.sync.dma_start(raw[:], w1[:, h * half : (h + 1) * half].rearrange("(p j) c -> p j c", j=PACK))
+            w1_raw.append(raw)
+            if h == 0:
+                for q in range(4):
+                    nc.sync.dma_start(scale_table[32 * q : 32 * q + 4, :].bitcast(I32), x_scales[0, 4 * q : 4 * q + 4, :].bitcast(I32))
+        nc.sync.dma_start(x_table[:], x_words[0].rearrange("p c r -> p (c r)").bitcast(I32))
+        nc.sync.dma_start(unit_sb[:], unit.rearrange("(p t) o -> p (t o)", t=PACK))
+        nc.sync.dma_start(el_sb[:], el)
+        nc.sync.dma_start(ct_sb[:], ct)
+        nc.sync.dma_start(nu_sb[:], nu)
+        w2_raw = keep.tile([P, PACK, N], F32, name="w2_raw")
+        nc.sync.dma_start(w2_raw[:], w2.rearrange("(p t) m -> p t m", t=PACK))
+
+        w1_grouped = keep.tile([P, PACK, P, PACK], BF16, name="w1_grouped", align_bytes=64)
+        for h in range(2):
+            dst = w1_grouped[:, :, h * 64 : (h + 1) * 64, :].rearrange("p t m j -> p m j t")
+            src = w1_raw[h][:].rearrange("p j (m t) -> p m j t", t=PACK)
+            if h == 0:
+                nc.scalar.copy(dst, src)
+            else:
+                nc.vector.tensor_copy(dst, src)
+        w1_codes = keep.tile([P, H], U32, name="w1_codes", align_bytes=64)
+        w1_scales = keep.tile([P, H], U8, name="w1_scales", align_bytes=64)
+        nc.vector.quantize_mx(out=w1_codes[:].bitcast(FP8X4), scales=w1_scales[:], in_=w1_grouped[:].rearrange("p t m j -> p (t m j)"))
+
+        x_bytes = keep.tile([P, S], U8, name="x_bytes", align_bytes=64)
+        nc.vector.tensor_copy(x_bytes[:], scale_table[:].indirect(offs_sb[:]))
+        x_codes = keep.tile([P, S], U32, name="x_codes", align_bytes=64)
+        nc.vector.tensor_copy(x_codes[:], x_table[:].bitcast(U32).indirect(offs_sb[:]))
+
+        unit_safe = keep.tile([P, PACK], F32, name="unit_safe")
+        nc.vector.scalar_tensor_tensor(unit_safe[:], unit_sb[:], 0.0, unit_sb[:], ALU.is_equal, ALU.add)
+        unit_inv = keep.tile([P, PACK], F32, name="unit_inv")
+        nc.vector.reciprocal(unit_inv[:], unit_safe[:])
+
+        w2_grouped = keep.tile([P, N, PACK], BF16, name="w2_grouped", align_bytes=64)
+        nc.scalar.copy(
+            w2_grouped[:].rearrange("p (c i) t -> p c t i", i=4),
+            w2_raw[:].rearrange("p t (c i) -> p c t i", i=4),
+        )
+        w2_codes = keep.tile([P, N], U32, name="w2_codes", align_bytes=64)
+        w2_scales = keep.tile([P, N], U8, name="w2_scales", align_bytes=64)
+
+        site = []
+        damp = []
+        for t in range(PACK):
+            bank = psum.tile([P, S], F32, name="y_bank%d" % t)
+            cols = slice(t * P, (t + 1) * P)
+            nc.tensor.matmul_mx(
+                out=bank[:],
+                lhsT=w1_codes[:, cols].bitcast(FP8X4),
+                lhsT_scale=w1_scales[:, cols],
+                rhs=x_codes[:].bitcast(FP8X4),
+                rhs_scale=x_bytes[:],
+                start=True,
+                stop=True,
+            )
+            size = keep.tile([P, S], F32, name="size%d" % t)
+            nc.scalar.activation(size[:], bank[:], ACT.Abs)
+            scaled = keep.tile([P, S], F32, name="site%d" % t)
+            nc.vector.tensor_scalar(scaled[:], bank[:], unit_sb[:, t : t + 1], None, ALU.mult)
+            root = keep.tile([P, S], F32, name="root%d" % t)
+            nc.scalar.activation(root[:], size[:], ACT.Abs_reciprocal_sqrt, bias=0.6)
+            recip = keep.tile([P, S], F32, name="damp%d" % t)
+            nc.vector.scalar_tensor_tensor(recip[:], root[:], unit_inv[:, t : t + 1], root[:], ALU.mult, ALU.mult)
+            site.append(scaled)
+            damp.append(recip)
+
+        nc.vector.quantize_mx(out=w2_codes[:].bitcast(FP8X4), scales=w2_scales[:], in_=w2_grouped[:].rearrange("p m t -> p (m t)"))
+
+        start = 0
+        for c, n in enumerate(CHUNKS):
+            lists = slice(start // 16, (start + n) // 16)
+            pairs = work.tile([P, 2, n, 2], BF16, name="pairs", align_bytes=64)
+            for u in range(2):
+                taker = work.tile([P, 2, n], F32, name="taker%d" % u)
+                giver = work.tile([P, 2, n], F32, name="giver%d" % u)
+                ratio = work.tile([P, 2, n], F32, name="ratio%d" % u)
+                for e in range(2):
+                    t = 2 * u + e
+                    if (c, t) in VECTOR_GATHERS:
+                        nc.vector.tensor_copy(taker[:, e, :], site[t][:].indirect(el_sb[:, lists]))
+                    else:
+                        nc.scalar.activation(taker[:, e, :], site[t][:].indirect(el_sb[:, lists]), ACT.Copy)
+                    nc.scalar.activation(giver[:, e, :], site[t][:].indirect(nu_sb[:, lists]), ACT.Copy)
+                    nc.vector.tensor_tensor(ratio[:, e, :], damp[t][:].indirect(ct_sb[:, lists]), taker[:, e, :], ALU.mult)
+                nc.vector.scalar_tensor_tensor(
+                    pairs[:, u, :, :],
+                    ratio[:].rearrange("p e r -> p r e"),
+                    1.0,
+                    giver[:].rearrange("p e r -> p r e"),
+                    ALU.subtract,
+                    ALU.mult,
+                )
+            hid = work.tile([P, n, PACK], BF16, name="hid", align_bytes=64)
+            nc.vector.tensor_copy(
+                hid[:].rearrange("p r t -> p (r t)").bitcast(I32).rearrange("p (r u) -> p r u", u=2),
+                pairs[:].rearrange("p u r e -> p (u r e)").bitcast(I32).rearrange("p (u r) -> p r u", u=2),
+            )
+            hid_codes = work.tile([P, n], U32, name="hid_codes", align_bytes=64)
+            hid_scales = work.tile([P, n], U8, name="hid_scales", align_bytes=64)
+            nc.vector.quantize_mx(out=hid_codes[:].bitcast(FP8X4), scales=hid_scales[:], in_=hid[:].rearrange("p r t -> p (r t)"))
+            acc = psum.tile([P, n], F32, name="out_bank%d" % c)
+            at = 0
+            for width in MM_WIDTHS[n]:
+                cols = slice(at, at + width)
+                nc.tensor.matmul_mx(
+                    out=acc[:, cols],
+                    lhsT=w2_codes[:].bitcast(FP8X4),
+                    lhsT_scale=w2_scales[:],
+                    rhs=hid_codes[:, cols].bitcast(FP8X4),
+                    rhs_scale=hid_scales[:, cols],
+                    start=True,
+                    stop=True,
+                )
+                at = at + width
+            result = work.tile([P, n], F32, name="result")
+            nc.vector.tensor_copy(result[:], acc[:])
+            nc.sync.dma_start(out[:, start : start + n], result[:])
+            start = start + n

@@ -17,16 +17,16 @@ ACT = mybir.ActivationFunctionType
 
 P = 128
 PACK = 4
-CHUNKS = (384, 384, 128, 128)
-MM_WIDTHS = {384: (256, 128), 256: (256,), 128: (128,)}
-VECTOR_GATHERS = ((0, 0),)
+CHUNKS = (512, 256, 128, 128)
+WINDOW = U + 16
+VECTOR_SHARE = 896
 
 
 def tile_picked_ypartnr_cat_p_kernel(tc, x_words, x_scales, w1, unit, w2, offs, nu, el, ct, out):
     nc = tc.nc
     with ExitStack() as ctx:
         keep = ctx.enter_context(tc.tile_pool(name="keep", bufs=1))
-        work = ctx.enter_context(tc.tile_pool(name="work", bufs=2))
+        work = ctx.enter_context(tc.tile_pool(name="work", bufs=4))
         psum = ctx.enter_context(tc.psum_pool(name="psum", bufs=1))
 
         offs_sb = keep.tile([P, S // 16], U16, name="offs_sb")
@@ -38,6 +38,12 @@ def tile_picked_ypartnr_cat_p_kernel(tc, x_words, x_scales, w1, unit, w2, offs, 
         unit_sb = keep.tile([P, PACK], F32, name="unit_sb")
 
         nc.vector.memset(scale_table[:].bitcast(I32), 0)
+        site = [keep.tile([P, WINDOW], F32, name="site%d" % t) for t in range(PACK)]
+        damp = [keep.tile([P, WINDOW], F32, name="damp%d" % t) for t in range(PACK)]
+        for window in site + damp:
+            nc.gpsimd.memset(window[:, U:WINDOW], 0.0)
+        warm = keep.tile([P, 1], F32, name="warm")
+        nc.scalar.activation(warm[:], site[0][:, U : U + 1], ACT.Abs_reciprocal_sqrt, bias=0.6)
         nc.sync.dma_start(offs_sb[:], offs)
         half = H // 2
         w1_raw = []
@@ -71,7 +77,8 @@ def tile_picked_ypartnr_cat_p_kernel(tc, x_words, x_scales, w1, unit, w2, offs, 
         x_bytes = keep.tile([P, S], U8, name="x_bytes", align_bytes=64)
         nc.vector.tensor_copy(x_bytes[:], scale_table[:].indirect(offs_sb[:]))
         x_codes = keep.tile([P, S], U32, name="x_codes", align_bytes=64)
-        nc.vector.tensor_copy(x_codes[:], x_table[:].bitcast(U32).indirect(offs_sb[:]))
+        for h in range(2):
+            nc.vector.tensor_copy(x_codes[:, h * 256 : (h + 1) * 256], x_table[:].bitcast(U32).indirect(offs_sb[:, h * 16 : (h + 1) * 16]))
 
         unit_safe = keep.tile([P, PACK], F32, name="unit_safe")
         nc.vector.scalar_tensor_tensor(unit_safe[:], unit_sb[:], 0.0, unit_sb[:], ALU.is_equal, ALU.add)
@@ -86,80 +93,107 @@ def tile_picked_ypartnr_cat_p_kernel(tc, x_words, x_scales, w1, unit, w2, offs, 
         w2_codes = keep.tile([P, N], U32, name="w2_codes", align_bytes=64)
         w2_scales = keep.tile([P, N], U8, name="w2_scales", align_bytes=64)
 
-        site = []
-        damp = []
-        for t in range(PACK):
-            bank = psum.tile([P, S], F32, name="y_bank%d" % t)
+        def first_product(t, lo, hi, tag):
+            bank = psum.tile([P, hi - lo], F32, name="y_bank", tag=tag)
             cols = slice(t * P, (t + 1) * P)
             nc.tensor.matmul_mx(
                 out=bank[:],
                 lhsT=w1_codes[:, cols].bitcast(FP8X4),
                 lhsT_scale=w1_scales[:, cols],
-                rhs=x_codes[:].bitcast(FP8X4),
-                rhs_scale=x_bytes[:],
+                rhs=x_codes[:, lo:hi].bitcast(FP8X4),
+                rhs_scale=x_bytes[:, lo:hi],
                 start=True,
                 stop=True,
             )
-            size = keep.tile([P, S], F32, name="size%d" % t)
-            nc.scalar.activation(size[:], bank[:], ACT.Abs)
-            scaled = keep.tile([P, S], F32, name="site%d" % t)
-            nc.vector.tensor_scalar(scaled[:], bank[:], unit_sb[:, t : t + 1], None, ALU.mult)
-            root = keep.tile([P, S], F32, name="root%d" % t)
-            nc.scalar.activation(root[:], size[:], ACT.Abs_reciprocal_sqrt, bias=0.6)
-            recip = keep.tile([P, S], F32, name="damp%d" % t)
-            nc.vector.scalar_tensor_tensor(recip[:], root[:], unit_inv[:, t : t + 1], root[:], ALU.mult, ALU.mult)
-            site.append(scaled)
-            damp.append(recip)
+            return (t, lo, hi, bank)
 
+        early = [first_product(t, h * 256, (h + 1) * 256, "bank%d" % (2 * h + t)) for h in range(2) for t in (0, 1)]
+        late = [first_product(t, 0, S, "bank%d" % (2 + t)) for t in (2, 3)]
         nc.vector.quantize_mx(out=w2_codes[:].bitcast(FP8X4), scales=w2_scales[:], in_=w2_grouped[:].rearrange("p m t -> p (m t)"))
 
-        start = 0
+        def magnitudes(banks, tiles):
+            for t, lo, hi, bank in banks:
+                nc.scalar.activation(site[t][:, S + lo : S + hi], bank[:], ACT.Abs)
+            for t in tiles:
+                nc.scalar.activation(damp[t][:, S:U], site[t][:, S:U], ACT.Abs_reciprocal_sqrt, bias=0.6)
+
+        def windows(banks, tiles):
+            for t, lo, hi, bank in banks:
+                nc.vector.tensor_scalar(site[t][:, lo:hi], bank[:], unit_sb[:, t : t + 1], None, ALU.mult)
+            for t in tiles:
+                root = damp[t][:, S:U]
+                nc.vector.scalar_tensor_tensor(damp[t][:, 0:S], root, unit_inv[:, t : t + 1], root, ALU.mult, ALU.mult)
+
+        taker = [keep.tile([P, 2, U], F32, name="taker%d" % u) for u in range(2)]
+        giver = [keep.tile([P, 2, U], F32, name="giver%d" % u) for u in range(2)]
+        ratio = [keep.tile([P, 2, U], F32, name="ratio%d" % u) for u in range(2)]
+        pairs = [keep.tile([P, 2, 2 * n], BF16, name="pairs%d" % c, align_bytes=64) for c, n in enumerate(CHUNKS)]
+        starts = [sum(CHUNKS[:c]) for c in range(len(CHUNKS))]
+
+        def entries(lst, lo, hi):
+            return lst[:, lo // 16 : hi // 16]
+
+        def fetch(dst, lst, t, lo, hi):
+            nc.scalar.activation(dst[t // 2][:, t % 2, lo:hi], site[t][:].indirect(entries(lst, lo, hi)), ACT.Copy)
+
+        def damped(t, lo, hi):
+            nc.vector.tensor_tensor(
+                ratio[t // 2][:, t % 2, lo:hi], damp[t][:].indirect(entries(ct_sb, lo, hi)), taker[t // 2][:, t % 2, lo:hi], ALU.mult
+            )
+
+        def finish_pair(u, c):
+            lo = starts[c]
+            hi = lo + CHUNKS[c]
+            nc.vector.scalar_tensor_tensor(
+                pairs[c][:, u, :].rearrange("p (r e) -> p r e", e=2),
+                ratio[u][:, :, lo:hi].rearrange("p e r -> p r e"),
+                1.0,
+                giver[u][:, :, lo:hi].rearrange("p e r -> p r e"),
+                ALU.subtract,
+                ALU.mult,
+            )
+
+        magnitudes(early, (0, 1))
+        windows(early, (0, 1))
+        nc.vector.tensor_copy(giver[0][:, 1, 0:VECTOR_SHARE], site[1][:].indirect(entries(nu_sb, 0, VECTOR_SHARE)))
+        for t in (0, 1):
+            fetch(taker, el_sb, t, 0, U)
+            damped(t, 0, U)
+        magnitudes(late, (2, 3))
+        windows(late, (2, 3))
+        for t in (2, 3):
+            fetch(taker, el_sb, t, 0, U)
+            damped(t, 0, U)
+        fetch(giver, nu_sb, 0, 0, U)
+        fetch(giver, nu_sb, 1, VECTOR_SHARE, U)
+        for c in range(len(CHUNKS)):
+            finish_pair(0, c)
+
+        lo = 0
         for c, n in enumerate(CHUNKS):
-            lists = slice(start // 16, (start + n) // 16)
-            pairs = work.tile([P, 2, n, 2], BF16, name="pairs", align_bytes=64)
-            for u in range(2):
-                taker = work.tile([P, 2, n], F32, name="taker%d" % u)
-                giver = work.tile([P, 2, n], F32, name="giver%d" % u)
-                ratio = work.tile([P, 2, n], F32, name="ratio%d" % u)
-                for e in range(2):
-                    t = 2 * u + e
-                    if (c, t) in VECTOR_GATHERS:
-                        nc.vector.tensor_copy(taker[:, e, :], site[t][:].indirect(el_sb[:, lists]))
-                    else:
-                        nc.scalar.activation(taker[:, e, :], site[t][:].indirect(el_sb[:, lists]), ACT.Copy)
-                    nc.scalar.activation(giver[:, e, :], site[t][:].indirect(nu_sb[:, lists]), ACT.Copy)
-                    nc.vector.tensor_tensor(ratio[:, e, :], damp[t][:].indirect(ct_sb[:, lists]), taker[:, e, :], ALU.mult)
-                nc.vector.scalar_tensor_tensor(
-                    pairs[:, u, :, :],
-                    ratio[:].rearrange("p e r -> p r e"),
-                    1.0,
-                    giver[:].rearrange("p e r -> p r e"),
-                    ALU.subtract,
-                    ALU.mult,
-                )
+            hi = lo + n
+            for t in (2, 3):
+                fetch(giver, nu_sb, t, lo, hi)
+            finish_pair(1, c)
             hid = work.tile([P, n, PACK], BF16, name="hid", align_bytes=64)
             nc.vector.tensor_copy(
                 hid[:].rearrange("p r t -> p (r t)").bitcast(I32).rearrange("p (r u) -> p r u", u=2),
-                pairs[:].rearrange("p u r e -> p (u r e)").bitcast(I32).rearrange("p (u r) -> p r u", u=2),
+                pairs[c][:].bitcast(I32).rearrange("p u r -> p r u"),
             )
             hid_codes = work.tile([P, n], U32, name="hid_codes", align_bytes=64)
             hid_scales = work.tile([P, n], U8, name="hid_scales", align_bytes=64)
             nc.vector.quantize_mx(out=hid_codes[:].bitcast(FP8X4), scales=hid_scales[:], in_=hid[:].rearrange("p r t -> p (r t)"))
-            acc = psum.tile([P, n], F32, name="out_bank%d" % c)
-            at = 0
-            for width in MM_WIDTHS[n]:
-                cols = slice(at, at + width)
-                nc.tensor.matmul_mx(
-                    out=acc[:, cols],
-                    lhsT=w2_codes[:].bitcast(FP8X4),
-                    lhsT_scale=w2_scales[:],
-                    rhs=hid_codes[:, cols].bitcast(FP8X4),
-                    rhs_scale=hid_scales[:, cols],
-                    start=True,
-                    stop=True,
-                )
-                at = at + width
+            acc = psum.tile([P, n], F32, name="out_bank", tag="bank%d" % ((6 + c) % 8))
+            nc.tensor.matmul_mx(
+                out=acc[:],
+                lhsT=w2_codes[:].bitcast(FP8X4),
+                lhsT_scale=w2_scales[:],
+                rhs=hid_codes[:].bitcast(FP8X4),
+                rhs_scale=hid_scales[:],
+                start=True,
+                stop=True,
+            )
             result = work.tile([P, n], F32, name="result")
-            nc.vector.tensor_copy(result[:], acc[:])
-            nc.sync.dma_start(out[:, start : start + n], result[:])
-            start = start + n
+            nc.scalar.copy(result[:], acc[:])
+            nc.sync.dma_start(out[:, lo:hi], result[:])
+            lo = hi

@@ -17,9 +17,10 @@ ACT = mybir.ActivationFunctionType
 
 P = 128
 PACK = 4
-CHUNKS = (512, 256, 128, 128)
+CHUNKS = (384, 256, 256, 128)
+MM_WIDTHS = {512: (512,), 384: (256, 128), 256: (256,), 128: (128,)}
+SCALAR_WEAVES = (1, 2)
 WINDOW = U + 16
-VECTOR_SHARE = 896
 
 
 def tile_picked_ypartnr_cat_p_kernel(tc, x_words, x_scales, w1, unit, w2, offs, nu, el, ct, out):
@@ -44,18 +45,15 @@ def tile_picked_ypartnr_cat_p_kernel(tc, x_words, x_scales, w1, unit, w2, offs, 
             nc.gpsimd.memset(window[:, U:WINDOW], 0.0)
         warm = keep.tile([P, 1], F32, name="warm")
         nc.scalar.activation(warm[:], site[0][:, U : U + 1], ACT.Abs_reciprocal_sqrt, bias=0.6)
+        w1_raw = keep.tile([P, PACK, H], F32, name="w1_raw")
+        w1_rows = w1.rearrange("(p j) c -> p j c", j=PACK)
         nc.sync.dma_start(offs_sb[:], offs)
-        half = H // 2
-        w1_raw = []
-        for h in range(2):
-            raw = keep.tile([P, PACK, half], F32, name="w1_raw%d" % h)
-            nc.sync.dma_start(raw[:], w1[:, h * half : (h + 1) * half].rearrange("(p j) c -> p j c", j=PACK))
-            w1_raw.append(raw)
-            if h == 0:
-                for q in range(4):
-                    nc.sync.dma_start(scale_table[32 * q : 32 * q + 4, :].bitcast(I32), x_scales[0, 4 * q : 4 * q + 4, :].bitcast(I32))
-        nc.sync.dma_start(x_table[:], x_words[0].rearrange("p c r -> p (c r)").bitcast(I32))
+        nc.sync.dma_start(w1_raw[:, 0:2, :], w1_rows[:, 0:2, :])
+        for q in range(4):
+            nc.sync.dma_start(scale_table[32 * q : 32 * q + 4, :].bitcast(I32), x_scales[0, 4 * q : 4 * q + 4, :].bitcast(I32))
+        nc.sync.dma_start(w1_raw[:, 2:4, :], w1_rows[:, 2:4, :])
         nc.sync.dma_start(unit_sb[:], unit.rearrange("(p t) o -> p (t o)", t=PACK))
+        nc.sync.dma_start(x_table[:], x_words[0].rearrange("p c r -> p (c r)").bitcast(I32))
         nc.sync.dma_start(el_sb[:], el)
         nc.sync.dma_start(ct_sb[:], ct)
         nc.sync.dma_start(nu_sb[:], nu)
@@ -65,7 +63,7 @@ def tile_picked_ypartnr_cat_p_kernel(tc, x_words, x_scales, w1, unit, w2, offs, 
         w1_grouped = keep.tile([P, PACK, P, PACK], BF16, name="w1_grouped", align_bytes=64)
         for h in range(2):
             dst = w1_grouped[:, :, h * 64 : (h + 1) * 64, :].rearrange("p t m j -> p m j t")
-            src = w1_raw[h][:].rearrange("p j (m t) -> p m j t", t=PACK)
+            src = w1_raw[:, :, h * 256 : (h + 1) * 256].rearrange("p j (m t) -> p m j t", t=PACK)
             if h == 0:
                 nc.scalar.copy(dst, src)
             else:
@@ -154,18 +152,18 @@ def tile_picked_ypartnr_cat_p_kernel(tc, x_words, x_scales, w1, unit, w2, offs, 
             )
 
         magnitudes(early, (0, 1))
-        windows(early, (0, 1))
-        nc.vector.tensor_copy(giver[0][:, 1, 0:VECTOR_SHARE], site[1][:].indirect(entries(nu_sb, 0, VECTOR_SHARE)))
+        windows(early + late, (0, 1))
+        for lo in (0, S):
+            nc.vector.tensor_copy(giver[0][:, 1, lo : lo + S], site[1][:].indirect(entries(nu_sb, lo, lo + S)))
         for t in (0, 1):
             fetch(taker, el_sb, t, 0, U)
             damped(t, 0, U)
         magnitudes(late, (2, 3))
-        windows(late, (2, 3))
+        windows((), (2, 3))
         for t in (2, 3):
             fetch(taker, el_sb, t, 0, U)
             damped(t, 0, U)
         fetch(giver, nu_sb, 0, 0, U)
-        fetch(giver, nu_sb, 1, VECTOR_SHARE, U)
         for c in range(len(CHUNKS)):
             finish_pair(0, c)
 
@@ -176,23 +174,28 @@ def tile_picked_ypartnr_cat_p_kernel(tc, x_words, x_scales, w1, unit, w2, offs, 
                 fetch(giver, nu_sb, t, lo, hi)
             finish_pair(1, c)
             hid = work.tile([P, n, PACK], BF16, name="hid", align_bytes=64)
-            nc.vector.tensor_copy(
-                hid[:].rearrange("p r t -> p (r t)").bitcast(I32).rearrange("p (r u) -> p r u", u=2),
-                pairs[c][:].bitcast(I32).rearrange("p u r -> p r u"),
+            weave, word = (nc.scalar.copy, U32) if c in SCALAR_WEAVES else (nc.vector.tensor_copy, I32)
+            weave(
+                hid[:].rearrange("p r t -> p (r t)").bitcast(word).rearrange("p (r u) -> p r u", u=2),
+                pairs[c][:].bitcast(word).rearrange("p u r -> p r u"),
             )
             hid_codes = work.tile([P, n], U32, name="hid_codes", align_bytes=64)
             hid_scales = work.tile([P, n], U8, name="hid_scales", align_bytes=64)
             nc.vector.quantize_mx(out=hid_codes[:].bitcast(FP8X4), scales=hid_scales[:], in_=hid[:].rearrange("p r t -> p (r t)"))
             acc = psum.tile([P, n], F32, name="out_bank", tag="bank%d" % ((6 + c) % 8))
-            nc.tensor.matmul_mx(
-                out=acc[:],
-                lhsT=w2_codes[:].bitcast(FP8X4),
-                lhsT_scale=w2_scales[:],
-                rhs=hid_codes[:].bitcast(FP8X4),
-                rhs_scale=hid_scales[:],
-                start=True,
-                stop=True,
-            )
+            at = 0
+            for width in MM_WIDTHS[n]:
+                cols = slice(at, at + width)
+                nc.tensor.matmul_mx(
+                    out=acc[:, cols],
+                    lhsT=w2_codes[:].bitcast(FP8X4),
+                    lhsT_scale=w2_scales[:],
+                    rhs=hid_codes[:, cols].bitcast(FP8X4),
+                    rhs_scale=hid_scales[:, cols],
+                    start=True,
+                    stop=True,
+                )
+                at = at + width
             result = work.tile([P, n], F32, name="result")
             nc.scalar.copy(result[:], acc[:])
             nc.sync.dma_start(out[:, lo:hi], result[:])

from contextlib import ExitStack

import concourse.mybir as mybir

K, T, S, N, H, U = 512, 2048, 512, 128, 512, 1024
FLOPS = 2 * K * H * S + 2 * H * N * U

F32 = mybir.dt.float32
BF16 = mybir.dt.bfloat16
I32 = mybir.dt.int32
U32 = mybir.dt.uint32
U16 = mybir.dt.uint16
U8 = mybir.dt.uint8
FP8X4 = mybir.dt.float8_e4m3fn_x4
ALU = mybir.AluOpType
ACT = mybir.ActivationFunctionType

P = 128
PACK = 4
CHUNKS = (384, 256, 256, 128)
MM_WIDTHS = {512: (512,), 384: (256, 128), 256: (256,), 128: (128,)}
SCALAR_WEAVES = (1, 2)
WINDOW = U + 16


def tile_picked_ypartnr_cat_p_kernel(tc, x_words, x_scales, w1, unit, w2, offs, nu, el, ct, out):
    nc = tc.nc
    with ExitStack() as ctx:
        keep = ctx.enter_context(tc.tile_pool(name="keep", bufs=1))
        work = ctx.enter_context(tc.tile_pool(name="work", bufs=4))
        psum = ctx.enter_context(tc.psum_pool(name="psum", bufs=1))

        offs_sb = keep.tile([P, S // 16], U16, name="offs_sb")
        nu_sb = keep.tile([P, U // 16], U16, name="nu_sb")
        el_sb = keep.tile([P, U // 16], U16, name="el_sb")
        ct_sb = keep.tile([P, U // 16], U16, name="ct_sb")
        x_table = keep.tile([P, T], I32, name="x_table", align_bytes=64)
        scale_table = keep.tile([P, T], U8, name="scale_table", align_bytes=64)
        unit_sb = keep.tile([P, PACK], F32, name="unit_sb")

        nc.vector.memset(scale_table[:].bitcast(I32), 0)
        site = [keep.tile([P, WINDOW], F32, name="site%d" % t) for t in range(PACK)]
        damp = [keep.tile([P, WINDOW], F32, name="damp%d" % t) for t in range(PACK)]
        for window in site + damp:
            nc.gpsimd.memset(window[:, U:WINDOW], 0.0)
        warm = keep.tile([P, 1], F32, name="warm")
        nc.scalar.activation(warm[:], site[0][:, U : U + 1], ACT.Abs_reciprocal_sqrt, bias=0.6)
        w1_raw = keep.tile([P, PACK, H], F32, name="w1_raw")
        w1_rows = w1.rearrange("(p j) c -> p j c", j=PACK)
        nc.sync.dma_start(offs_sb[:], offs)
        nc.sync.dma_start(w1_raw[:, 0:2, :], w1_rows[:, 0:2, :])
        for q in range(4):
            nc.sync.dma_start(scale_table[32 * q : 32 * q + 4, :].bitcast(I32), x_scales[0, 4 * q : 4 * q + 4, :].bitcast(I32))
        nc.sync.dma_start(w1_raw[:, 2:4, :], w1_rows[:, 2:4, :])
        nc.sync.dma_start(unit_sb[:], unit.rearrange("(p t) o -> p (t o)", t=PACK))
        nc.sync.dma_start(x_table[:], x_words[0].rearrange("p c r -> p (c r)").bitcast(I32))
        nc.sync.dma_start(el_sb[:], el)
        nc.sync.dma_start(ct_sb[:], ct)
        nc.sync.dma_start(nu_sb[:], nu)
        w2_raw = keep.tile([P, PACK, N], F32, name="w2_raw")
        nc.sync.dma_start(w2_raw[:], w2.rearrange("(p t) m -> p t m", t=PACK))

        w1_grouped = keep.tile([P, PACK, P, PACK], BF16, name="w1_grouped", align_bytes=64)
        for h in range(2):
            dst = w1_grouped[:, :, h * 64 : (h + 1) * 64, :].rearrange("p t m j -> p m j t")
            src = w1_raw[:, :, h * 256 : (h + 1) * 256].rearrange("p j (m t) -> p m j t", t=PACK)
            if h == 0:
                nc.scalar.copy(dst, src)
            else:
                nc.vector.tensor_copy(dst, src)
        w1_codes = keep.tile([P, H], U32, name="w1_codes", align_bytes=64)
        w1_scales = keep.tile([P, H], U8, name="w1_scales", align_bytes=64)
        nc.vector.quantize_mx(out=w1_codes[:].bitcast(FP8X4), scales=w1_scales[:], in_=w1_grouped[:].rearrange("p t m j -> p (t m j)"))

        x_bytes = keep.tile([P, S], U8, name="x_bytes", align_bytes=64)
        nc.vector.tensor_copy(x_bytes[:], scale_table[:].indirect(offs_sb[:]))
        x_codes = keep.tile([P, S], U32, name="x_codes", align_bytes=64)
        for h in range(2):
            nc.vector.tensor_copy(x_codes[:, h * 256 : (h + 1) * 256], x_table[:].bitcast(U32).indirect(offs_sb[:, h * 16 : (h + 1) * 16]))

        unit_safe = keep.tile([P, PACK], F32, name="unit_safe")
        nc.vector.scalar_tensor_tensor(unit_safe[:], unit_sb[:], 0.0, unit_sb[:], ALU.is_equal, ALU.add)
        unit_inv = keep.tile([P, PACK], F32, name="unit_inv")
        nc.vector.reciprocal(unit_inv[:], unit_safe[:])

        w2_grouped = keep.tile([P, N, PACK], BF16, name="w2_grouped", align_bytes=64)
        nc.scalar.copy(
            w2_grouped[:].rearrange("p (c i) t -> p c t i", i=4),
            w2_raw[:].rearrange("p t (c i) -> p c t i", i=4),
        )
        w2_codes = keep.tile([P, N], U32, name="w2_codes", align_bytes=64)
        w2_scales = keep.tile([P, N], U8, name="w2_scales", align_bytes=64)

        def first_product(t, lo, hi, tag):
            bank = psum.tile([P, hi - lo], F32, name="y_bank", tag=tag)
            cols = slice(t * P, (t + 1) * P)
            nc.tensor.matmul_mx(
                out=bank[:],
                lhsT=w1_codes[:, cols].bitcast(FP8X4),
                lhsT_scale=w1_scales[:, cols],
                rhs=x_codes[:, lo:hi].bitcast(FP8X4),
                rhs_scale=x_bytes[:, lo:hi],
                start=True,
                stop=True,
            )
            return (t, lo, hi, bank)

        early = [first_product(t, h * 256, (h + 1) * 256, "bank%d" % (2 * h + t)) for h in range(2) for t in (0, 1)]
        late = [first_product(t, 0, S, "bank%d" % (2 + t)) for t in (2, 3)]
        nc.vector.quantize_mx(out=w2_codes[:].bitcast(FP8X4), scales=w2_scales[:], in_=w2_grouped[:].rearrange("p m t -> p (m t)"))

        def magnitudes(banks, tiles):
            for t, lo, hi, bank in banks:
                nc.scalar.activation(site[t][:, S + lo : S + hi], bank[:], ACT.Abs)
            for t in tiles:
                nc.scalar.activation(damp[t][:, S:U], site[t][:, S:U], ACT.Abs_reciprocal_sqrt, bias=0.6)

        def windows(banks, tiles):
            for t, lo, hi, bank in banks:
                nc.vector.tensor_scalar(site[t][:, lo:hi], bank[:], unit_sb[:, t : t + 1], None, ALU.mult)
            for t in tiles:
                root = damp[t][:, S:U]
                nc.vector.scalar_tensor_tensor(damp[t][:, 0:S], root, unit_inv[:, t : t + 1], root, ALU.mult, ALU.mult)

        taker = [keep.tile([P, 2, U], F32, name="taker%d" % u) for u in range(2)]
        giver = [keep.tile([P, 2, U], F32, name="giver%d" % u) for u in range(2)]
        ratio = [keep.tile([P, 2, U], F32, name="ratio%d" % u) for u in range(2)]
        pairs = [keep.tile([P, 2, 2 * n], BF16, name="pairs%d" % c, align_bytes=64) for c, n in enumerate(CHUNKS)]
        starts = [sum(CHUNKS[:c]) for c in range(len(CHUNKS))]

        def entries(lst, lo, hi):
            return lst[:, lo // 16 : hi // 16]

        def fetch(dst, lst, t, lo, hi):
            nc.scalar.activation(dst[t // 2][:, t % 2, lo:hi], site[t][:].indirect(entries(lst, lo, hi)), ACT.Copy)

        def damped(t, lo, hi):
            nc.vector.tensor_tensor(
                ratio[t // 2][:, t % 2, lo:hi], damp[t][:].indirect(entries(ct_sb, lo, hi)), taker[t // 2][:, t % 2, lo:hi], ALU.mult
            )

        def finish_pair(u, c):
            lo = starts[c]
            hi = lo + CHUNKS[c]
            nc.vector.scalar_tensor_tensor(
                pairs[c][:, u, :].rearrange("p (r e) -> p r e", e=2),
                ratio[u][:, :, lo:hi].rearrange("p e r -> p r e"),
                1.0,
                giver[u][:, :, lo:hi].rearrange("p e r -> p r e"),
                ALU.subtract,
                ALU.mult,
            )

        magnitudes(early, (0, 1))
        windows(early + late, (0, 1))
        for lo in (0, S):
            nc.vector.tensor_copy(giver[0][:, 1, lo : lo + S], site[1][:].indirect(entries(nu_sb, lo, lo + S)))
        for t in (0, 1):
            fetch(taker, el_sb, t, 0, U)
            damped(t, 0, U)
        magnitudes(late, (2, 3))
        windows((), (2, 3))
        for t in (2, 3):
            fetch(taker, el_sb, t, 0, U)
            damped(t, 0, U)
        fetch(giver, nu_sb, 0, 0, U)
        for c in range(len(CHUNKS)):
            finish_pair(0, c)

        lo = 0
        for c, n in enumerate(CHUNKS):
            hi = lo + n
            for t in (2, 3):
                fetch(giver, nu_sb, t, lo, hi)
            finish_pair(1, c)
            hid = work.tile([P, n, PACK], BF16, name="hid", align_bytes=64)
            weave, word = (nc.scalar.copy, U32) if c in SCALAR_WEAVES else (nc.vector.tensor_copy, I32)
            weave(
                hid[:].rearrange("p r t -> p (r t)").bitcast(word).rearrange("p (r u) -> p r u", u=2),
                pairs[c][:].bitcast(word).rearrange("p u r -> p r u"),
            )
            hid_codes = work.tile([P, n], U32, name="hid_codes", align_bytes=64)
            hid_scales = work.tile([P, n], U8, name="hid_scales", align_bytes=64)
            nc.vector.quantize_mx(out=hid_codes[:].bitcast(FP8X4), scales=hid_scales[:], in_=hid[:].rearrange("p r t -> p (r t)"))
            acc = psum.tile([P, n], F32, name="out_bank", tag="bank%d" % ((6 + c) % 8))
            at = 0
            for width in MM_WIDTHS[n]:
                cols = slice(at, at + width)
                nc.tensor.matmul_mx(
                    out=acc[:, cols],
                    lhsT=w2_codes[:].bitcast(FP8X4),
                    lhsT_scale=w2_scales[:],
                    rhs=hid_codes[:, cols].bitcast(FP8X4),
                    rhs_scale=hid_scales[:, cols],
                    start=True,
                    stop=True,
                )
                at = at + width
            result = work.tile([P, n], F32, name="result")
            nc.scalar.copy(result[:], acc[:])
            nc.sync.dma_start(out[:, lo:hi], result[:])
            lo = hi
